import numpy as np
import ml_dtypes


def mxq(x, axis, fmt="e4m3"):
    dtype, down = {"e4m3": (ml_dtypes.float8_e4m3fn, 7), "e5m2": (ml_dtypes.float8_e5m2, 14)}[fmt]
    v = np.moveaxis(np.asarray(x, np.float32).astype(ml_dtypes.bfloat16).astype(np.float64), axis, -1)
    blocks = v.reshape(v.shape[:-1] + (-1, 32))
    amax = np.abs(blocks).max(-1, keepdims=True)
    byte = np.maximum(np.where(amax > 0, np.frexp(amax)[1] - 1 + 127, 0) - down, 1)
    scale = np.exp2(byte - 127.0)
    codes = (blocks / scale).astype(np.float32).astype(dtype).astype(np.float64)
    return np.moveaxis((codes * scale).reshape(v.shape), -1, axis)


WIDE = False


def mx_kscale(k):
    if not WIDE:
        return np.ones(k)
    levels = np.array([10, -10, 5, -5, 0])
    if k % 512:
        return np.exp2(np.random.permutation(np.resize(levels, k // 32))).repeat(32)
    a = np.empty((k // 512, 16))
    for p in range(k // 512):
        a[p, :8] = np.random.permutation(np.resize(levels, 8))
        for g in range(8):
            far = levels[np.abs(levels - a[p, g]) >= 10]
            a[p, g + 8] = far[np.random.randint(len(far))]
    return np.exp2(a.ravel()).repeat(32)


def f64(x):
    return np.asarray(x).astype(np.float64)


def striped(idx):
    return np.tile(idx.reshape(-1, 16).T, (8, 1)).astype(np.uint16)


def unstriped(offs):
    return offs[:16].T.reshape(-1).astype(np.int64)


def d_silu(v):
    s = 1.0 / (1.0 + np.exp(-np.maximum(v, -700.0)))
    return s * (1.0 + v * (1.0 - s))


K, T, E, C, H, N = 384, 1280, 2, 512, 256, 1024


def by_expert(wq, xq):
    return np.concatenate([wq[e].T @ xq[:, e * C:(e + 1) * C] for e in range(E)], axis=1)


def setup_inputs():
    n = np.random.standard_normal
    slot_token = np.random.permutation(T)[:E * C]
    s = mx_kscale(N)[:, None]
    z = np.ones(T); z[slot_token] = mx_kscale(E * C)
    return {
        "xT": (n((K, T)) * z[None, :]).astype(np.float32),
        "dyT": (n((N, T)) * s).astype(np.float32),
        "a": n((H, E * C)).astype(np.float32),
        "w2": (n((E, N, H)) / np.sqrt(N) / s[None]).astype(np.float32),
        "gate": np.tile(np.random.uniform(0.2, 1.0, E * C) / z[slot_token], (N, 1)).astype(np.float32),
        "offs": striped(slot_token),
    }


def reference(xT, dyT, a, w2, gate, offs):
    idx = unstriped(offs)
    gq = mxq(f64(gate) * f64(dyT)[:, idx], 0, "e4m3")
    dh = by_expert(mxq(f64(w2), 1, "e4m3"), gq)
    da = mxq(dh * d_silu(f64(a)), 1, "e4m3")
    xq = mxq(f64(xT)[:, idx], 1, "e4m3")
    return np.stack([(xq[:, e * C:(e + 1) * C] @ da[:, e * C:(e + 1) * C].T) for e in range(E)])

@@ -1,0 +1,305 @@
+from contextlib import ExitStack
+
+import concourse.mybir as mybir
+from concourse.masks import make_identity
+
+K, T, E, C, H, N = 384, 1280, 2, 512, 256, 1024
+P = 128
+PACK = 4
+FLOPS = 2 * E * C * H * (N + K)
+BYTES = 4 * (K * T + N * T + H * E * C + E * N * H + E * C + E * K * H) + 2 * P * E * C // 16
+
+F32 = mybir.dt.float32
+BF16 = mybir.dt.bfloat16
+U32 = mybir.dt.uint32
+U16 = mybir.dt.uint16
+U8 = mybir.dt.uint8
+FP8X4 = mybir.dt.float8_e4m3fn_x4
+ACT = mybir.ActivationFunctionType
+ALU = mybir.AluOpType
+
+
+def tile_moe_mlp_silu_kernel(tc, xT, dyT, a, w2, gate, offs, out):
+    nc = tc.nc
+    with ExitStack() as ctx:
+        held = ctx.enter_context(tc.tile_pool(name="held", bufs=1))
+        psum = ctx.enter_context(tc.psum_pool(name="psum", bufs=1))
+
+        def sb(shape, dtype, name):
+            return held.tile(shape, dtype, name=name, tag=name, align_bytes=64)
+
+        def bank(name, tag):
+            return psum.tile([P, 512], F32, name=name, tag=tag)
+
+        offsets = sb([P, E * C // 16], U16, "offsets")
+        dy = {(c, j): sb([P, T], F32, "dy%d%d" % (c, j)) for c in range(2) for j in range(PACK)}
+        gates = sb([P, E * C], F32, "gates")
+        x32 = [sb([P, T], F32, "x32_%d" % b) for b in range(3)]
+        x16 = [sb([P, T], BF16, "x16_%d" % b) for b in range(3)]
+        xs = [sb([P, E, C], BF16, "xs%d" % b) for b in range(3)]
+        xg = [sb([P, E * P * 2], F32, "xg%d" % b) for b in range(3)]
+        x_codes = [sb([P, E * P], U32, "xc%d" % b) for b in range(3)]
+        x_scales = [sb([P, E * P], U8, "xsc%d" % b) for b in range(3)]
+        w32 = {(e, c): sb([P, PACK, H], F32, "w32_%d%d" % (e, c)) for e in range(E) for c in range(2)}
+        wg = {(e, c): sb([P, H * PACK], BF16, "wg%d%d" % (e, c)) for e in range(E) for c in range(2)}
+        w_codes = {(e, c): sb([P, H], U32, "wc%d%d" % (e, c)) for e in range(E) for c in range(2)}
+        w_scales = {(e, c): sb([P, H], U8, "wsc%d%d" % (e, c)) for e in range(E) for c in range(2)}
+        g32 = [sb([P, PACK, E * C], F32, "g32_%d" % c) for c in range(2)]
+        gg = {(e, c): sb([P, C * PACK], BF16, "gg%d%d" % (e, c)) for e in range(E) for c in range(2)}
+        g_codes = {(e, c): sb([P, C], U32, "gc%d%d" % (e, c)) for e in range(E) for c in range(2)}
+        g_scales = {(e, c): sb([P, C], U8, "gsc%d%d" % (e, c)) for e in range(E) for c in range(2)}
+        a32 = sb([P, 2, E * C], F32, "a32")
+        sig = sb([P, 2, E * C], F32, "sig")
+        sil = sb([P, 2, E * C], F32, "sil")
+        negd = sb([P, 2, E * C], F32, "negd")
+        da = {(e, i): sb([P, C], BF16, "da%d%d" % (e, i)) for e in range(E) for i in range(2)}
+        dag = [sb([P, H * 2], F32, "dag%d" % e) for e in range(E)]
+        da_codes = [sb([P, H], U32, "dac%d" % e) for e in range(E)]
+        da_scales = [sb([P, H], U8, "dasc%d" % e) for e in range(E)]
+        gate_row = sb([P, 8], F32, "gate_row")
+        gate_rep = [sb([P, 4, P], F32, "gate_rep%d" % half) for half in range(2)]
+        acc = {}
+        ident = sb([P, P], F32, "ident")
+        warm_in = sb([P, 1], F32, "warm_in")
+        warm_out = sb([P, 1], F32, "warm_out")
+        dh = {}
+
+        dy_rows = dyT.rearrange("(c p j) t -> c j p t", c=2, j=PACK)
+        w_rows = w2.rearrange("e (c p j) i -> e c p j i", c=2, j=PACK)
+
+        def load_dy(c, j):
+            nc.sync.dma_start(dy[c, j][:], dy_rows[c, j])
+
+        def load_gate(e):
+            nc.sync.dma_start(gates[:, e * C:(e + 1) * C], gate[0:P, e * C:(e + 1) * C])
+
+        def load_x(b):
+            nc.sync.dma_start(x32[b][:], xT[b * P:(b + 1) * P, :])
+
+        def load_w(e, c):
+            nc.sync.dma_start(w32[e, c][:], w_rows[e, c])
+
+        def load_a(i):
+            nc.sync.dma_start(a32[:, i, :], a[i * P:(i + 1) * P, :])
+
+        def copy_on(engine, dst, src):
+            if engine == "v":
+                nc.vector.tensor_copy(dst, src)
+            else:
+                nc.scalar.copy(dst, src)
+
+        def quantize(codes, scales, src):
+            nc.vector.quantize_mx(out=codes.bitcast(FP8X4), scales=scales, in_=src)
+
+        def gather_g(c, j, lo, hi):
+            nc.vector.tensor_tensor(
+                g32[c][:, j, lo:hi], dy[c, j][:].indirect(offsets[:, lo // 16:hi // 16]), gates[:, lo:hi], ALU.mult)
+
+        def interleave(engine, dst, src):
+            copy_on(engine, dst.rearrange("p (m r j) -> p m j r", r=4, j=PACK),
+                    src.rearrange("p j (m r) -> p m j r", r=4))
+
+        def group_g(engine, e, c, lo=0, hi=C):
+            interleave(engine, gg[e, c][:, lo * PACK:hi * PACK], g32[c][:, :, e * C + lo:e * C + hi])
+
+        def quant_g(e, c, lo=0, hi=C):
+            quantize(g_codes[e, c][:, lo:hi], g_scales[e, c][:, lo:hi], gg[e, c][:, lo * PACK:hi * PACK])
+
+        def group_w(engine, e, c):
+            interleave(engine, wg[e, c][:], w32[e, c][:])
+
+        def quant_w(e, c):
+            quantize(w_codes[e, c][:], w_scales[e, c][:], wg[e, c][:])
+
+        def cast_x(engine, b):
+            copy_on(engine, x16[b][:], x32[b][:])
+
+        def gather_x(b, e):
+            nc.scalar.activation(
+                xs[b][:, e, :].rearrange("p (u m) -> p m u", u=2),
+                x16[b][:].indirect(offsets[:, e * C // 16:(e + 1) * C // 16]), ACT.Copy)
+
+        def turn_x(engine, b, tag):
+            turned = bank("xt%d" % b, tag)
+            words = xs[b][:].rearrange("p e s -> p (e s)").bitcast(F32)
+            for q in range(4):
+                nc.tensor.transpose(turned[:, q * P:(q + 1) * P], words[:, q * P:(q + 1) * P], ident[:])
+            copy_on(engine, xg[b][:].rearrange("p (e k u) -> p e k u", e=E, u=2),
+                    turned[:].rearrange("p (e u k) -> p e k u", e=E, u=2))
+
+        def quant_x(b):
+            quantize(x_codes[b][:], x_scales[b][:], xg[b][:].bitcast(BF16))
+
+        def sigmoid():
+            nc.scalar.activation(sig[:], a32[:], ACT.Sigmoid)
+
+        def silu_neg(e):
+            nc.scalar.activation(sil[:, :, e * C:(e + 1) * C], a32[:, :, e * C:(e + 1) * C], ACT.Silu, scale=-1.0)
+
+        def dsilu(e):
+            cols = slice(e * C, (e + 1) * C)
+            nc.vector.scalar_tensor_tensor(negd[:, :, cols], sil[:, :, cols], 1.0, sig[:, :, cols], ALU.subtract, ALU.mult)
+
+        def mm_dh(e, c, i, lo, hi, tag, at):
+            if (tag, e) not in dh:
+                dh[tag, e] = bank("dh%s%d" % (tag, e), tag)
+            nc.tensor.matmul_mx(
+                out=dh[tag, e][:, at:at + hi - lo], lhsT=w_codes[e, c][:, i * P:(i + 1) * P].bitcast(FP8X4),
+                lhsT_scale=w_scales[e, c][:, i * P:(i + 1) * P],
+                rhs=g_codes[e, c][:, lo:hi].bitcast(FP8X4), rhs_scale=g_scales[e, c][:, lo:hi],
+                start=(c == 0), stop=(c == 1))
+
+        def make_da(e, i, lo, hi, tag, at):
+            nc.vector.scalar_tensor_tensor(
+                da[e, i][:].rearrange("p (u m) -> p u m", u=2)[:, :, lo // 2:hi // 2],
+                dh[tag, e][:, at:at + hi - lo].rearrange("p (m u) -> p u m", u=2), -1.0,
+                negd[:, i, e * C + lo:e * C + hi].rearrange("p (m u) -> p u m", u=2), ALU.mult, ALU.mult)
+
+        def turn_da_half(engine, e, i, tag):
+            turned = bank("dat%d%d" % (e, i), tag)
+            words = da[e, i][:].bitcast(F32)
+            for u in range(2):
+                nc.tensor.transpose(turned[:, u * P:(u + 1) * P], words[:, u * P:(u + 1) * P], ident[:])
+            copy_on(engine, dag[e][:, i * 2 * P:(i + 1) * 2 * P].rearrange("p (k u) -> p k u", u=2),
+                    turned[:, 0:2 * P].rearrange("p (u k) -> p k u", u=2))
+
+        def turn_da(engine, e, tag):
+            turned = bank("dat%d" % e, tag)
+            for i in range(2):
+                words = da[e, i][:].bitcast(F32)
+                for u in range(2):
+                    q = 2 * i + u
+                    nc.tensor.transpose(turned[:, q * P:(q + 1) * P], words[:, u * P:(u + 1) * P], ident[:])
+            copy_on(engine, dag[e][:].rearrange("p (i k u) -> p i k u", i=2, u=2),
+                    turned[:].rearrange("p (i u k) -> p i k u", i=2, u=2))
+
+        def quant_da(e):
+            quantize(da_codes[e][:], da_scales[e][:], dag[e][:].bitcast(BF16))
+
+        def out_mm(e, b, tag, at):
+            if (tag, e) not in acc:
+                acc[tag, e] = bank("acc%s%d" % (tag, e), tag)
+            nc.tensor.matmul_mx(
+                out=acc[tag, e][:, at:at + H], lhsT=x_codes[b][:, e * P:(e + 1) * P].bitcast(FP8X4),
+                lhsT_scale=x_scales[b][:, e * P:(e + 1) * P],
+                rhs=da_codes[e][:].bitcast(FP8X4), rhs_scale=da_scales[e][:], start=True, stop=True)
+
+        def out_store(engine, e, b, count, tag):
+            res = sb([P, count, H], F32, "res%d%d" % (e, b))
+            copy_on(engine, res[:].rearrange("p b i -> p (b i)"), acc[tag, e][:, 0:count * H])
+            nc.sync.dma_start(out[e, b * P:(b + count) * P, :].rearrange("(b p) i -> p b i", b=count), res[:])
+
+        def load_gate_row():
+            nc.sync.dma_start(gate_row[:], gate[0, :].rearrange("(p m) -> p m", m=8))
+
+        def repeat_gate(half):
+            nc.vector.tensor_copy(gate_rep[half][:], gate_row[:, 4 * half:4 * half + 4].unsqueeze(2).to_broadcast([P, 4, P]))
+
+        def spread_gate(engine, half, tag):
+            spread = bank("spread%d" % half, tag)
+            for m in range(4):
+                nc.tensor.transpose(spread[:, m * P:(m + 1) * P], gate_rep[half][:, m, :], ident[:])
+            copy_on(engine, gates[:].rearrange("q (p h m) -> q h p m", h=2, m=4)[:, half],
+                    spread[:].rearrange("q (m p) -> q p m", m=4))
+
+        load_gate_row()
+        nc.sync.dma_start(offsets[:], offs)
+        load_x(0)
+        load_dy(1, 3)
+        load_dy(0, 1)
+        load_a(1)
+        load_a(0)
+        load_dy(1, 2)
+        load_dy(0, 2)
+        load_dy(1, 0)
+        load_dy(0, 3)
+        load_w(0, 1)
+        load_x(1)
+        load_w(1, 0)
+        load_x(2)
+        load_w(0, 0)
+        load_dy(0, 0)
+        load_dy(1, 1)
+        load_w(1, 1)
+        nc.vector.memset(warm_in[:], 0.0)
+        nc.scalar.activation(warm_out[:], warm_in[:], ACT.Sigmoid)
+        make_identity(nc, ident[:])
+        group_w("s", 1, 0)
+        repeat_gate(1)
+        group_w("s", 0, 0)
+        sigmoid()
+        spread_gate("s", 1, "b1")
+        repeat_gate(0)
+        silu_neg(1)
+        spread_gate("v", 0, "b0")
+        gather_g(1, 1, 0, 1024)
+        silu_neg(0)
+        dsilu(0)
+        gather_g(1, 3, 0, 512)
+        group_w("s", 0, 1)
+        gather_g(1, 2, 0, 1024)
+        gather_g(0, 1, 0, 1024)
+        group_w("s", 1, 1)
+        cast_x("v", 0)
+        quant_w(0, 0)
+        gather_g(1, 0, 0, 1024)
+        gather_g(0, 2, 0, 1024)
+        cast_x("s", 2)
+        gather_g(1, 3, 512, 1024)
+        gather_g(0, 0, 0, 1024)
+        gather_g(0, 3, 0, 1024)
+        group_g("v", 0, 0)
+        quant_g(0, 0)
+        gather_x(2, 0)
+        gather_x(0, 0)
+        group_g("s", 0, 1, 256, 512)
+        mm_dh(0, 0, 1, 0, 512, "b1", 0)
+        group_g("v", 0, 1, 0, 256)
+        group_g("v", 1, 1, 0, 256)
+        quant_g(0, 1)
+        gather_x(0, 1)
+        group_g("s", 1, 1, 256, 512)
+        dsilu(1)
+        group_g("s", 1, 0)
+        quant_g(1, 0)
+        cast_x("s", 1)
+        mm_dh(0, 0, 0, 0, 512, "b0", 0)
+        gather_x(1, 0)
+        gather_x(2, 1)
+        quant_w(1, 0)
+        quant_w(1, 1)
+        gather_x(1, 1)
+        quant_w(0, 1)
+        turn_x("s", 0, "b6")
+        mm_dh(0, 1, 0, 0, 512, "b0", 0)
+        make_da(0, 0, 0, 512, "b0", 0)
+        turn_x("s", 2, "b4")
+        mm_dh(0, 1, 1, 0, 512, "b1", 0)
+        mm_dh(1, 0, 0, 0, 512, "b2", 0)
+        quant_g(1, 1)
+        make_da(0, 1, 0, 512, "b1", 0)
+        mm_dh(1, 1, 0, 0, 512, "b2", 0)
+        quant_x(0)
+        mm_dh(1, 0, 1, 0, 512, "b3", 0)
+        quant_x(2)
+        make_da(1, 0, 0, 512, "b2", 0)
+        turn_da("s", 0, "b5")
+        mm_dh(1, 1, 1, 0, 512, "b3", 0)
+        turn_x("s", 1, "b7")
+        make_da(1, 1, 0, 512, "b3", 0)
+        turn_da_half("s", 1, 0, "b4")
+        turn_da_half("s", 1, 1, "b5")
+        quant_da(0)
+        out_mm(0, 2, "b7", 0)
+        quant_da(1)
+        out_mm(1, 2, "b2", 0)
+        out_mm(0, 0, "b6", 0)
+        out_mm(1, 0, "b0", 0)
+        quant_x(1)
+        out_mm(0, 1, "b6", 256)
+        out_store("s", 1, 2, 1, "b2")
+        out_store("s", 0, 0, 2, "b6")
+        out_mm(1, 1, "b1", 0)
+        out_store("v", 0, 2, 1, "b7")
+        out_store("v", 1, 1, 1, "b1")
+        out_store("s", 1, 0, 1, "b0")

@@ -25,8 +25,8 @@ def tile_moe_mlp_silu_kernel(tc, xT, dyT, a, w2, gate, offs, out):
         held = ctx.enter_context(tc.tile_pool(name="held", bufs=1))
         psum = ctx.enter_context(tc.psum_pool(name="psum", bufs=1))
 
-        def sb(shape, dtype, name):
-            return held.tile(shape, dtype, name=name, tag=name, align_bytes=64)
+        def sb(shape, dtype, name, tag=None):
+            return held.tile(shape, dtype, name=name, tag=tag or name, align_bytes=64)
 
         def bank(name, tag):
             return psum.tile([P, 512], F32, name=name, tag=tag)
@@ -38,11 +38,10 @@ def tile_moe_mlp_silu_kernel(tc, xT, dyT, a, w2, gate, offs, out):
         x16 = [sb([P, T], BF16, "x16_%d" % b) for b in range(3)]
         xs = [sb([P, E, C], BF16, "xs%d" % b) for b in range(3)]
         xg = [sb([P, E * P * 2], F32, "xg%d" % b) for b in range(3)]
-        x_codes = [sb([P, E * P], U32, "xc%d" % b) for b in range(3)]
+        late = {}
         x_scales = [sb([P, E * P], U8, "xsc%d" % b) for b in range(3)]
         w32 = {(e, c): sb([P, PACK, H], F32, "w32_%d%d" % (e, c)) for e in range(E) for c in range(2)}
         wg = {(e, c): sb([P, H * PACK], BF16, "wg%d%d" % (e, c)) for e in range(E) for c in range(2)}
-        w_codes = {(e, c): sb([P, H], U32, "wc%d%d" % (e, c)) for e in range(E) for c in range(2)}
         w_scales = {(e, c): sb([P, H], U8, "wsc%d%d" % (e, c)) for e in range(E) for c in range(2)}
         g32 = [sb([P, PACK, E * C], F32, "g32_%d" % c) for c in range(2)]
         gg = {(e, c): sb([P, C * PACK], BF16, "gg%d%d" % (e, c)) for e in range(E) for c in range(2)}
@@ -51,7 +50,6 @@ def tile_moe_mlp_silu_kernel(tc, xT, dyT, a, w2, gate, offs, out):
         a32 = sb([P, 2, E * C], F32, "a32")
         sig = sb([P, 2, E * C], F32, "sig")
         sil = sb([P, 2, E * C], F32, "sil")
-        negd = sb([P, 2, E * C], F32, "negd")
         da = {(e, i): sb([P, C], BF16, "da%d%d" % (e, i)) for e in range(E) for i in range(2)}
         dag = [sb([P, H * 2], F32, "dag%d" % e) for e in range(E)]
         da_codes = [sb([P, H], U32, "dac%d" % e) for e in range(E)]
@@ -82,6 +80,16 @@ def tile_moe_mlp_silu_kernel(tc, xT, dyT, a, w2, gate, offs, out):
         def load_a(i):
             nc.sync.dma_start(a32[:, i, :], a[i * P:(i + 1) * P, :])
 
+        def after_gathers(last):
+            late["negd"] = sb([P, 2, E * C], F32, "negd", "gates")
+            late["codes"] = sb([P, 7 * H], U32, "codes", last)
+
+        def w_code(e, c):
+            return late["codes"][:, (2 * e + c) * H:(2 * e + c + 1) * H]
+
+        def x_code(b):
+            return late["codes"][:, (4 + b) * H:(5 + b) * H]
+
         def copy_on(engine, dst, src):
             if engine == "v":
                 nc.vector.tensor_copy(dst, src)
@@ -109,7 +117,7 @@ def tile_moe_mlp_silu_kernel(tc, xT, dyT, a, w2, gate, offs, out):
             interleave(engine, wg[e, c][:], w32[e, c][:])
 
         def quant_w(e, c):
-            quantize(w_codes[e, c][:], w_scales[e, c][:], wg[e, c][:])
+            quantize(w_code(e, c), w_scales[e, c][:], wg[e, c][:])
 
         def cast_x(engine, b):
             copy_on(engine, x16[b][:], x32[b][:])
@@ -128,7 +136,7 @@ def tile_moe_mlp_silu_kernel(tc, xT, dyT, a, w2, gate, offs, out):
                     turned[:].rearrange("p (e u k) -> p e k u", e=E, u=2))
 
         def quant_x(b):
-            quantize(x_codes[b][:], x_scales[b][:], xg[b][:].bitcast(BF16))
+            quantize(x_code(b), x_scales[b][:], xg[b][:].bitcast(BF16))
 
         def sigmoid():
             nc.scalar.activation(sig[:], a32[:], ACT.Sigmoid)
@@ -138,13 +146,13 @@ def tile_moe_mlp_silu_kernel(tc, xT, dyT, a, w2, gate, offs, out):
 
         def dsilu(e):
             cols = slice(e * C, (e + 1) * C)
-            nc.vector.scalar_tensor_tensor(negd[:, :, cols], sil[:, :, cols], 1.0, sig[:, :, cols], ALU.subtract, ALU.mult)
+            nc.vector.scalar_tensor_tensor(late["negd"][:, :, cols], sil[:, :, cols], 1.0, sig[:, :, cols], ALU.subtract, ALU.mult)
 
         def mm_dh(e, c, i, lo, hi, tag, at):
             if (tag, e) not in dh:
                 dh[tag, e] = bank("dh%s%d" % (tag, e), tag)
             nc.tensor.matmul_mx(
-                out=dh[tag, e][:, at:at + hi - lo], lhsT=w_codes[e, c][:, i * P:(i + 1) * P].bitcast(FP8X4),
+                out=dh[tag, e][:, at:at + hi - lo], lhsT=w_code(e, c)[:, i * P:(i + 1) * P].bitcast(FP8X4),
                 lhsT_scale=w_scales[e, c][:, i * P:(i + 1) * P],
                 rhs=g_codes[e, c][:, lo:hi].bitcast(FP8X4), rhs_scale=g_scales[e, c][:, lo:hi],
                 start=(c == 0), stop=(c == 1))
@@ -153,7 +161,7 @@ def tile_moe_mlp_silu_kernel(tc, xT, dyT, a, w2, gate, offs, out):
             nc.vector.scalar_tensor_tensor(
                 da[e, i][:].rearrange("p (u m) -> p u m", u=2)[:, :, lo // 2:hi // 2],
                 dh[tag, e][:, at:at + hi - lo].rearrange("p (m u) -> p u m", u=2), -1.0,
-                negd[:, i, e * C + lo:e * C + hi].rearrange("p (m u) -> p u m", u=2), ALU.mult, ALU.mult)
+                late["negd"][:, i, e * C + lo:e * C + hi].rearrange("p (m u) -> p u m", u=2), ALU.mult, ALU.mult)
 
         def turn_da_half(engine, e, i, tag):
             turned = bank("dat%d%d" % (e, i), tag)
@@ -180,7 +188,7 @@ def tile_moe_mlp_silu_kernel(tc, xT, dyT, a, w2, gate, offs, out):
             if (tag, e) not in acc:
                 acc[tag, e] = bank("acc%s%d" % (tag, e), tag)
             nc.tensor.matmul_mx(
-                out=acc[tag, e][:, at:at + H], lhsT=x_codes[b][:, e * P:(e + 1) * P].bitcast(FP8X4),
+                out=acc[tag, e][:, at:at + H], lhsT=x_code(b)[:, e * P:(e + 1) * P].bitcast(FP8X4),
                 lhsT_scale=x_scales[b][:, e * P:(e + 1) * P],
                 rhs=da_codes[e][:].bitcast(FP8X4), rhs_scale=da_scales[e][:], start=True, stop=True)
 
@@ -202,104 +210,103 @@ def tile_moe_mlp_silu_kernel(tc, xT, dyT, a, w2, gate, offs, out):
             copy_on(engine, gates[:].rearrange("q (p h m) -> q h p m", h=2, m=4)[:, half],
                     spread[:].rearrange("q (m p) -> q p m", m=4))
 
-        load_gate_row()
         nc.sync.dma_start(offsets[:], offs)
-        load_x(0)
-        load_dy(1, 3)
-        load_dy(0, 1)
-        load_a(1)
-        load_a(0)
-        load_dy(1, 2)
-        load_dy(0, 2)
-        load_dy(1, 0)
-        load_dy(0, 3)
-        load_w(0, 1)
-        load_x(1)
-        load_w(1, 0)
-        load_x(2)
-        load_w(0, 0)
         load_dy(0, 0)
+        load_gate(0)
+        load_gate(1)
+        load_dy(1, 2)
+        load_x(1)
+        load_dy(1, 0)
+        load_a(1)
         load_dy(1, 1)
+        load_a(0)
+        load_dy(0, 1)
+        load_dy(0, 3)
+        load_w(0, 0)
+        load_dy(0, 2)
+        load_w(1, 0)
         load_w(1, 1)
+        load_dy(1, 3)
+        load_x(2)
+        load_w(0, 1)
+        load_x(0)
         nc.vector.memset(warm_in[:], 0.0)
         nc.scalar.activation(warm_out[:], warm_in[:], ACT.Sigmoid)
         make_identity(nc, ident[:])
-        group_w("s", 1, 0)
-        repeat_gate(1)
         group_w("s", 0, 0)
-        sigmoid()
-        spread_gate("s", 1, "b1")
-        repeat_gate(0)
-        silu_neg(1)
-        spread_gate("v", 0, "b0")
-        gather_g(1, 1, 0, 1024)
-        silu_neg(0)
-        dsilu(0)
-        gather_g(1, 3, 0, 512)
-        group_w("s", 0, 1)
         gather_g(1, 2, 0, 1024)
-        gather_g(0, 1, 0, 1024)
-        group_w("s", 1, 1)
-        cast_x("v", 0)
-        quant_w(0, 0)
-        gather_g(1, 0, 0, 1024)
-        gather_g(0, 2, 0, 1024)
-        cast_x("s", 2)
-        gather_g(1, 3, 512, 1024)
-        gather_g(0, 0, 0, 1024)
-        gather_g(0, 3, 0, 1024)
-        group_g("v", 0, 0)
-        quant_g(0, 0)
-        gather_x(2, 0)
-        gather_x(0, 0)
-        group_g("s", 0, 1, 256, 512)
-        mm_dh(0, 0, 1, 0, 512, "b1", 0)
-        group_g("v", 0, 1, 0, 256)
-        group_g("v", 1, 1, 0, 256)
-        quant_g(0, 1)
-        gather_x(0, 1)
-        group_g("s", 1, 1, 256, 512)
-        dsilu(1)
-        group_g("s", 1, 0)
-        quant_g(1, 0)
         cast_x("s", 1)
-        mm_dh(0, 0, 0, 0, 512, "b0", 0)
+        gather_g(0, 3, 0, 1024)
+        gather_g(0, 0, 512, 1024)
+        gather_g(1, 1, 0, 1024)
+        gather_g(1, 0, 0, 1024)
+        group_w("s", 1, 0)
+        gather_g(0, 2, 0, 1024)
         gather_x(1, 0)
-        gather_x(2, 1)
-        quant_w(1, 0)
-        quant_w(1, 1)
-        gather_x(1, 1)
+        gather_g(0, 1, 0, 1024)
+        gather_g(1, 3, 0, 512)
+        cast_x("s", 2)
+        sigmoid()
+        gather_g(0, 0, 0, 512)
+        group_g("s", 0, 0)
+        gather_g(1, 3, 512, 1024)
+        after_gathers("dy13")
+        group_g("v", 1, 0)
+        quant_g(0, 0)
+        group_g("s", 0, 1, 256, 512)
+        quant_w(0, 0)
+        mm_dh(0, 0, 0, 0, 512, "b0", 0)
+        silu_neg(0)
+        group_g("s", 1, 1, 256, 512)
+        group_g("s", 1, 1, 0, 256)
+        group_g("v", 0, 1, 0, 256)
+        gather_x(2, 0)
+        group_w("v", 0, 1)
         quant_w(0, 1)
-        turn_x("s", 0, "b6")
+        gather_x(1, 1)
+        quant_w(1, 0)
+        mm_dh(0, 0, 1, 0, 512, "b1", 0)
+        group_w("v", 1, 1)
+        quant_g(1, 1)
+        quant_g(1, 0)
+        quant_g(0, 1)
+        dsilu(0)
+        turn_x("s", 1, "b7")
+        silu_neg(1)
+        quant_w(1, 1)
+        mm_dh(1, 0, 0, 0, 512, "b2", 0)
+        mm_dh(1, 0, 1, 0, 512, "b3", 0)
+        mm_dh(1, 1, 1, 0, 512, "b3", 0)
+        gather_x(2, 1)
+        mm_dh(0, 1, 1, 0, 512, "b1", 0)
+        cast_x("v", 0)
+        mm_dh(1, 1, 0, 0, 512, "b2", 0)
+        gather_x(0, 0)
         mm_dh(0, 1, 0, 0, 512, "b0", 0)
         make_da(0, 0, 0, 512, "b0", 0)
-        turn_x("s", 2, "b4")
-        mm_dh(0, 1, 1, 0, 512, "b1", 0)
-        mm_dh(1, 0, 0, 0, 512, "b2", 0)
-        quant_g(1, 1)
+        gather_x(0, 1)
         make_da(0, 1, 0, 512, "b1", 0)
-        mm_dh(1, 1, 0, 0, 512, "b2", 0)
-        quant_x(0)
-        mm_dh(1, 0, 1, 0, 512, "b3", 0)
-        quant_x(2)
-        make_da(1, 0, 0, 512, "b2", 0)
+        dsilu(1)
         turn_da("s", 0, "b5")
-        mm_dh(1, 1, 1, 0, 512, "b3", 0)
-        turn_x("s", 1, "b7")
+        make_da(1, 0, 0, 512, "b2", 0)
         make_da(1, 1, 0, 512, "b3", 0)
-        turn_da_half("s", 1, 0, "b4")
-        turn_da_half("s", 1, 1, "b5")
+        turn_x("v", 2, "b4")
+        quant_x(2)
+        turn_da_half("s", 1, 0, "b0")
         quant_da(0)
-        out_mm(0, 2, "b7", 0)
+        turn_da_half("s", 1, 1, "b5")
+        turn_x("s", 0, "b6")
+        quant_x(0)
         quant_da(1)
-        out_mm(1, 2, "b2", 0)
         out_mm(0, 0, "b6", 0)
-        out_mm(1, 0, "b0", 0)
         quant_x(1)
-        out_mm(0, 1, "b6", 256)
-        out_store("s", 1, 2, 1, "b2")
-        out_store("s", 0, 0, 2, "b6")
+        out_mm(1, 0, "b3", 0)
         out_mm(1, 1, "b1", 0)
-        out_store("v", 0, 2, 1, "b7")
+        out_mm(1, 2, "b2", 0)
+        out_store("s", 1, 0, 1, "b3")
+        out_mm(0, 1, "b6", 256)
+        out_mm(0, 2, "b7", 0)
+        out_store("s", 0, 0, 2, "b6")
+        out_store("s", 1, 2, 1, "b2")
         out_store("v", 1, 1, 1, "b1")
-        out_store("s", 1, 0, 1, "b0")
+        out_store("s", 0, 2, 1, "b7")

from contextlib import ExitStack

import concourse.mybir as mybir
from concourse.masks import make_identity

K, T, E, C, H, N = 384, 1280, 2, 512, 256, 1024
P = 128
PACK = 4
FLOPS = 2 * E * C * H * (N + K)
BYTES = 4 * (K * T + N * T + H * E * C + E * N * H + E * C + E * K * H) + 2 * P * E * C // 16

F32 = mybir.dt.float32
BF16 = mybir.dt.bfloat16
U32 = mybir.dt.uint32
U16 = mybir.dt.uint16
U8 = mybir.dt.uint8
FP8X4 = mybir.dt.float8_e4m3fn_x4
ACT = mybir.ActivationFunctionType
ALU = mybir.AluOpType


def tile_moe_mlp_silu_kernel(tc, xT, dyT, a, w2, gate, offs, out):
    nc = tc.nc
    with ExitStack() as ctx:
        held = ctx.enter_context(tc.tile_pool(name="held", bufs=1))
        psum = ctx.enter_context(tc.psum_pool(name="psum", bufs=1))

        def sb(shape, dtype, name, tag=None):
            return held.tile(shape, dtype, name=name, tag=tag or name, align_bytes=64)

        def bank(name, tag):
            return psum.tile([P, 512], F32, name=name, tag=tag)

        offsets = sb([P, E * C // 16], U16, "offsets")
        dy = {(c, j): sb([P, T], F32, "dy%d%d" % (c, j)) for c in range(2) for j in range(PACK)}
        gates = sb([P, E * C], F32, "gates")
        x32 = [sb([P, T], F32, "x32_%d" % b) for b in range(3)]
        x16 = [sb([P, T], BF16, "x16_%d" % b) for b in range(3)]
        xs = [sb([P, E, C], BF16, "xs%d" % b) for b in range(3)]
        xg = [sb([P, E * P * 2], F32, "xg%d" % b) for b in range(3)]
        late = {}
        x_scales = [sb([P, E * P], U8, "xsc%d" % b) for b in range(3)]
        w32 = {(e, c): sb([P, PACK, H], F32, "w32_%d%d" % (e, c)) for e in range(E) for c in range(2)}
        wg = {(e, c): sb([P, H * PACK], BF16, "wg%d%d" % (e, c)) for e in range(E) for c in range(2)}
        w_scales = {(e, c): sb([P, H], U8, "wsc%d%d" % (e, c)) for e in range(E) for c in range(2)}
        g32 = [sb([P, PACK, E * C], F32, "g32_%d" % c) for c in range(2)]
        gg = {(e, c): sb([P, C * PACK], BF16, "gg%d%d" % (e, c)) for e in range(E) for c in range(2)}
        g_codes = {(e, c): sb([P, C], U32, "gc%d%d" % (e, c)) for e in range(E) for c in range(2)}
        g_scales = {(e, c): sb([P, C], U8, "gsc%d%d" % (e, c)) for e in range(E) for c in range(2)}
        a32 = sb([P, 2, E * C], F32, "a32")
        sig = sb([P, 2, E * C], F32, "sig")
        sil = sb([P, 2, E * C], F32, "sil")
        da = {(e, i): sb([P, C], BF16, "da%d%d" % (e, i)) for e in range(E) for i in range(2)}
        dag = [sb([P, H * 2], F32, "dag%d" % e) for e in range(E)]
        da_codes = [sb([P, H], U32, "dac%d" % e) for e in range(E)]
        da_scales = [sb([P, H], U8, "dasc%d" % e) for e in range(E)]
        gate_row = sb([P, 8], F32, "gate_row")
        gate_rep = [sb([P, 4, P], F32, "gate_rep%d" % half) for half in range(2)]
        acc = {}
        ident = sb([P, P], F32, "ident")
        warm_in = sb([P, 1], F32, "warm_in")
        warm_out = sb([P, 1], F32, "warm_out")
        dh = {}

        dy_rows = dyT.rearrange("(c p j) t -> c j p t", c=2, j=PACK)
        w_rows = w2.rearrange("e (c p j) i -> e c p j i", c=2, j=PACK)

        def load_dy(c, j):
            nc.sync.dma_start(dy[c, j][:], dy_rows[c, j])

        def load_gate(e):
            nc.sync.dma_start(gates[:, e * C:(e + 1) * C], gate[0:P, e * C:(e + 1) * C])

        def load_x(b):
            nc.sync.dma_start(x32[b][:], xT[b * P:(b + 1) * P, :])

        def load_w(e, c):
            nc.sync.dma_start(w32[e, c][:], w_rows[e, c])

        def load_a(i):
            nc.sync.dma_start(a32[:, i, :], a[i * P:(i + 1) * P, :])

        def after_gathers(last):
            late["negd"] = sb([P, 2, E * C], F32, "negd", "gates")
            late["codes"] = sb([P, 7 * H], U32, "codes", last)

        def w_code(e, c):
            return late["codes"][:, (2 * e + c) * H:(2 * e + c + 1) * H]

        def x_code(b):
            return late["codes"][:, (4 + b) * H:(5 + b) * H]

        def copy_on(engine, dst, src):
            if engine == "v":
                nc.vector.tensor_copy(dst, src)
            else:
                nc.scalar.copy(dst, src)

        def quantize(codes, scales, src):
            nc.vector.quantize_mx(out=codes.bitcast(FP8X4), scales=scales, in_=src)

        def gather_g(c, j, lo, hi):
            nc.vector.tensor_tensor(
                g32[c][:, j, lo:hi], dy[c, j][:].indirect(offsets[:, lo // 16:hi // 16]), gates[:, lo:hi], ALU.mult)

        def interleave(engine, dst, src):
            copy_on(engine, dst.rearrange("p (m r j) -> p m j r", r=4, j=PACK),
                    src.rearrange("p j (m r) -> p m j r", r=4))

        def group_g(engine, e, c, lo=0, hi=C):
            interleave(engine, gg[e, c][:, lo * PACK:hi * PACK], g32[c][:, :, e * C + lo:e * C + hi])

        def quant_g(e, c, lo=0, hi=C):
            quantize(g_codes[e, c][:, lo:hi], g_scales[e, c][:, lo:hi], gg[e, c][:, lo * PACK:hi * PACK])

        def group_w(engine, e, c):
            interleave(engine, wg[e, c][:], w32[e, c][:])

        def quant_w(e, c):
            quantize(w_code(e, c), w_scales[e, c][:], wg[e, c][:])

        def cast_x(engine, b):
            copy_on(engine, x16[b][:], x32[b][:])

        def gather_x(b, e):
            nc.scalar.activation(
                xs[b][:, e, :].rearrange("p (u m) -> p m u", u=2),
                x16[b][:].indirect(offsets[:, e * C // 16:(e + 1) * C // 16]), ACT.Copy)

        def turn_x(engine, b, tag):
            turned = bank("xt%d" % b, tag)
            words = xs[b][:].rearrange("p e s -> p (e s)").bitcast(F32)
            for q in range(4):
                nc.tensor.transpose(turned[:, q * P:(q + 1) * P], words[:, q * P:(q + 1) * P], ident[:])
            copy_on(engine, xg[b][:].rearrange("p (e k u) -> p e k u", e=E, u=2),
                    turned[:].rearrange("p (e u k) -> p e k u", e=E, u=2))

        def quant_x(b):
            quantize(x_code(b), x_scales[b][:], xg[b][:].bitcast(BF16))

        def sigmoid():
            nc.scalar.activation(sig[:], a32[:], ACT.Sigmoid)

        def silu_neg(e):
            nc.scalar.activation(sil[:, :, e * C:(e + 1) * C], a32[:, :, e * C:(e + 1) * C], ACT.Silu, scale=-1.0)

        def dsilu(e):
            cols = slice(e * C, (e + 1) * C)
            nc.vector.scalar_tensor_tensor(late["negd"][:, :, cols], sil[:, :, cols], 1.0, sig[:, :, cols], ALU.subtract, ALU.mult)

        def mm_dh(e, c, i, lo, hi, tag, at):
            if (tag, e) not in dh:
                dh[tag, e] = bank("dh%s%d" % (tag, e), tag)
            nc.tensor.matmul_mx(
                out=dh[tag, e][:, at:at + hi - lo], lhsT=w_code(e, c)[:, i * P:(i + 1) * P].bitcast(FP8X4),
                lhsT_scale=w_scales[e, c][:, i * P:(i + 1) * P],
                rhs=g_codes[e, c][:, lo:hi].bitcast(FP8X4), rhs_scale=g_scales[e, c][:, lo:hi],
                start=(c == 0), stop=(c == 1))

        def make_da(e, i, lo, hi, tag, at):
            nc.vector.scalar_tensor_tensor(
                da[e, i][:].rearrange("p (u m) -> p u m", u=2)[:, :, lo // 2:hi // 2],
                dh[tag, e][:, at:at + hi - lo].rearrange("p (m u) -> p u m", u=2), -1.0,
                late["negd"][:, i, e * C + lo:e * C + hi].rearrange("p (m u) -> p u m", u=2), ALU.mult, ALU.mult)

        def turn_da_half(engine, e, i, tag):
            turned = bank("dat%d%d" % (e, i), tag)
            words = da[e, i][:].bitcast(F32)
            for u in range(2):
                nc.tensor.transpose(turned[:, u * P:(u + 1) * P], words[:, u * P:(u + 1) * P], ident[:])
            copy_on(engine, dag[e][:, i * 2 * P:(i + 1) * 2 * P].rearrange("p (k u) -> p k u", u=2),
                    turned[:, 0:2 * P].rearrange("p (u k) -> p k u", u=2))

        def turn_da(engine, e, tag):
            turned = bank("dat%d" % e, tag)
            for i in range(2):
                words = da[e, i][:].bitcast(F32)
                for u in range(2):
                    q = 2 * i + u
                    nc.tensor.transpose(turned[:, q * P:(q + 1) * P], words[:, u * P:(u + 1) * P], ident[:])
            copy_on(engine, dag[e][:].rearrange("p (i k u) -> p i k u", i=2, u=2),
                    turned[:].rearrange("p (i u k) -> p i k u", i=2, u=2))

        def quant_da(e):
            quantize(da_codes[e][:], da_scales[e][:], dag[e][:].bitcast(BF16))

        def out_mm(e, b, tag, at):
            if (tag, e) not in acc:
                acc[tag, e] = bank("acc%s%d" % (tag, e), tag)
            nc.tensor.matmul_mx(
                out=acc[tag, e][:, at:at + H], lhsT=x_code(b)[:, e * P:(e + 1) * P].bitcast(FP8X4),
                lhsT_scale=x_scales[b][:, e * P:(e + 1) * P],
                rhs=da_codes[e][:].bitcast(FP8X4), rhs_scale=da_scales[e][:], start=True, stop=True)

        def out_store(engine, e, b, count, tag):
            res = sb([P, count, H], F32, "res%d%d" % (e, b))
            copy_on(engine, res[:].rearrange("p b i -> p (b i)"), acc[tag, e][:, 0:count * H])
            nc.sync.dma_start(out[e, b * P:(b + count) * P, :].rearrange("(b p) i -> p b i", b=count), res[:])

        def load_gate_row():
            nc.sync.dma_start(gate_row[:], gate[0, :].rearrange("(p m) -> p m", m=8))

        def repeat_gate(half):
            nc.vector.tensor_copy(gate_rep[half][:], gate_row[:, 4 * half:4 * half + 4].unsqueeze(2).to_broadcast([P, 4, P]))

        def spread_gate(engine, half, tag):
            spread = bank("spread%d" % half, tag)
            for m in range(4):
                nc.tensor.transpose(spread[:, m * P:(m + 1) * P], gate_rep[half][:, m, :], ident[:])
            copy_on(engine, gates[:].rearrange("q (p h m) -> q h p m", h=2, m=4)[:, half],
                    spread[:].rearrange("q (m p) -> q p m", m=4))

        nc.sync.dma_start(offsets[:], offs)
        load_dy(0, 0)
        load_gate(0)
        load_gate(1)
        load_dy(1, 2)
        load_x(1)
        load_dy(1, 0)
        load_a(1)
        load_dy(1, 1)
        load_a(0)
        load_dy(0, 1)
        load_dy(0, 3)
        load_w(0, 0)
        load_dy(0, 2)
        load_w(1, 0)
        load_w(1, 1)
        load_dy(1, 3)
        load_x(2)
        load_w(0, 1)
        load_x(0)
        nc.vector.memset(warm_in[:], 0.0)
        nc.scalar.activation(warm_out[:], warm_in[:], ACT.Sigmoid)
        make_identity(nc, ident[:])
        group_w("s", 0, 0)
        gather_g(1, 2, 0, 1024)
        cast_x("s", 1)
        gather_g(0, 3, 0, 1024)
        gather_g(0, 0, 512, 1024)
        gather_g(1, 1, 0, 1024)
        gather_g(1, 0, 0, 1024)
        group_w("s", 1, 0)
        gather_g(0, 2, 0, 1024)
        gather_x(1, 0)
        gather_g(0, 1, 0, 1024)
        gather_g(1, 3, 0, 512)
        cast_x("s", 2)
        sigmoid()
        gather_g(0, 0, 0, 512)
        group_g("s", 0, 0)
        gather_g(1, 3, 512, 1024)
        after_gathers("dy13")
        group_g("v", 1, 0)
        quant_g(0, 0)
        group_g("s", 0, 1, 256, 512)
        quant_w(0, 0)
        mm_dh(0, 0, 0, 0, 512, "b0", 0)
        silu_neg(0)
        group_g("s", 1, 1, 256, 512)
        group_g("s", 1, 1, 0, 256)
        group_g("v", 0, 1, 0, 256)
        gather_x(2, 0)
        group_w("v", 0, 1)
        quant_w(0, 1)
        gather_x(1, 1)
        quant_w(1, 0)
        mm_dh(0, 0, 1, 0, 512, "b1", 0)
        group_w("v", 1, 1)
        quant_g(1, 1)
        quant_g(1, 0)
        quant_g(0, 1)
        dsilu(0)
        turn_x("s", 1, "b7")
        silu_neg(1)
        quant_w(1, 1)
        mm_dh(1, 0, 0, 0, 512, "b2", 0)
        mm_dh(1, 0, 1, 0, 512, "b3", 0)
        mm_dh(1, 1, 1, 0, 512, "b3", 0)
        gather_x(2, 1)
        mm_dh(0, 1, 1, 0, 512, "b1", 0)
        cast_x("v", 0)
        mm_dh(1, 1, 0, 0, 512, "b2", 0)
        gather_x(0, 0)
        mm_dh(0, 1, 0, 0, 512, "b0", 0)
        make_da(0, 0, 0, 512, "b0", 0)
        gather_x(0, 1)
        make_da(0, 1, 0, 512, "b1", 0)
        dsilu(1)
        turn_da("s", 0, "b5")
        make_da(1, 0, 0, 512, "b2", 0)
        make_da(1, 1, 0, 512, "b3", 0)
        turn_x("v", 2, "b4")
        quant_x(2)
        turn_da_half("s", 1, 0, "b0")
        quant_da(0)
        turn_da_half("s", 1, 1, "b5")
        turn_x("s", 0, "b6")
        quant_x(0)
        quant_da(1)
        out_mm(0, 0, "b6", 0)
        quant_x(1)
        out_mm(1, 0, "b3", 0)
        out_mm(1, 1, "b1", 0)
        out_mm(1, 2, "b2", 0)
        out_store("s", 1, 0, 1, "b3")
        out_mm(0, 1, "b6", 256)
        out_mm(0, 2, "b7", 0)
        out_store("s", 0, 0, 2, "b6")
        out_store("s", 1, 2, 1, "b2")
        out_store("v", 1, 1, 1, "b1")
        out_store("s", 0, 2, 1, "b7")
